import numpy as np
import ml_dtypes


def mxq(x, axis, fmt="e4m3"):
    dtype, down = {"e4m3": (ml_dtypes.float8_e4m3fn, 7), "e5m2": (ml_dtypes.float8_e5m2, 14)}[fmt]
    v = np.moveaxis(np.asarray(x, np.float32).astype(ml_dtypes.bfloat16).astype(np.float64), axis, -1)
    blocks = v.reshape(v.shape[:-1] + (-1, 32))
    amax = np.abs(blocks).max(-1, keepdims=True)
    byte = np.maximum(np.where(amax > 0, np.frexp(amax)[1] - 1 + 127, 0) - down, 1)
    scale = np.exp2(byte - 127.0)
    codes = (blocks / scale).astype(np.float32).astype(dtype).astype(np.float64)
    return np.moveaxis((codes * scale).reshape(v.shape), -1, axis)


WIDE = False


def mx_kscale(k):
    if not WIDE:
        return np.ones(k)
    levels = np.array([30, -30])
    if k % 512:
        return np.exp2(np.random.permutation(np.resize(levels, k // 32))).repeat(32)
    a = np.empty((k // 512, 16))
    for p in range(k // 512):
        a[p, :8] = np.random.permutation(np.resize(levels, 8))
        for g in range(8):
            far = levels[np.abs(levels - a[p, g]) >= 10]
            a[p, g + 8] = far[np.random.randint(len(far))]
    return np.exp2(a.ravel()).repeat(32)


def f64(x):
    return np.asarray(x).astype(np.float64)


def striped(idx):
    return np.tile(np.asarray(idx).reshape(-1, 16).T, (8, 1)).astype(np.uint16)


def unstriped(offs):
    return offs[:16].T.reshape(-1).astype(np.int64)


E2M1 = np.array([0.0, 0.5, 1.0, 1.5, 2.0, 3.0, 4.0, 6.0, -0.0, -0.5, -1.0, -1.5, -2.0, -3.0, -4.0, -6.0])


def pack_weight(w, fmt):
    k, n = w.shape
    w = f64(np.asarray(w, np.float32).astype(ml_dtypes.bfloat16)).reshape(k // 32, 32, n)
    amax = np.abs(w).max(1)
    if fmt in ("e4m3", "e5m2"):
        byte = np.frexp(amax)[1] - 1 + 127 - (7 if fmt == "e4m3" else 14)
    else:
        mant, ex = np.frexp(amax / 6.0)
        byte = np.where(mant > 0.5, ex, ex - 1) + 127
    byte = np.clip(np.where(amax > 0, byte, 1), 1, 254)
    scaled = (w * np.exp2(127.0 - byte)[:, None, :]).reshape(k, n).astype(np.float32)
    by_word = np.ascontiguousarray(scaled.reshape(k // 512, 128, 4, n).transpose(0, 1, 3, 2))
    if fmt in ("e4m3", "e5m2"):
        words = by_word.astype(ml_dtypes.float8_e4m3fn if fmt == "e4m3" else ml_dtypes.float8_e5m2).view(np.uint8)
    else:
        c = by_word.astype(ml_dtypes.float4_e2m1fn).view(np.uint8) & 0xF
        words = (c[..., 0::2] | (c[..., 1::2] << 4)).reshape(k // 512, 128, 2 * n)
    return np.ascontiguousarray(words), np.ascontiguousarray(byte.astype(np.uint8).reshape(k // 512, 16, n))


def unpack_weight(words, scales, fmt):
    g, _, n = scales.shape
    words = np.ascontiguousarray(words).reshape(g, 128, n, -1)
    if fmt in ("e4m3", "e5m2"):
        vals = words.view(ml_dtypes.float8_e4m3fn if fmt == "e4m3" else ml_dtypes.float8_e5m2).astype(np.float64)
    else:
        nib = np.empty((g, 128, n, 4), np.uint8)
        nib[..., 0::2] = words & 0xF
        nib[..., 1::2] = words >> 4
        vals = E2M1[nib]
    vals = vals * np.repeat(np.exp2(scales.astype(np.float64) - 127.0), 8, axis=1)[..., None]
    return vals.transpose(0, 1, 3, 2).reshape(g * 512, n)


def e4m3fn_bytes(y):
    return np.clip(np.asarray(y, np.float64), -448.0, 448.0).astype(np.float32).astype(ml_dtypes.float8_e4m3fn).view(np.uint8)


def e4m3fn_values(b):
    return np.asarray(b, np.uint8).view(ml_dtypes.float8_e4m3fn).astype(np.float64)


K, T, J, R, F, Z, V, D, N = 512, 1024, 256, 512, 512, 1024, 1024, 512, 256


def setup_inputs():
    n = np.random.standard_normal
    idx = np.random.permutation(T)[:J]
    idx2 = np.random.permutation(Z)[:J]
    idx3 = np.random.permutation(V)[:J]
    idx4 = np.random.permutation(D)[:J]
    fk = mx_kscale(K)
    ff = mx_kscale(F)
    fr = mx_kscale(R)
    xtp = pack_weight(n((K, T)) / fk[:, None], "e5m2")
    xop = pack_weight(n((F, Z)) / ff[:, None], "e4m3")
    wp = pack_weight(n((K, R)) * 1 / np.sqrt(K) * fk[:, None], "e2m1")
    w2p = pack_weight(n((F, R)) * 1 / np.sqrt(F) * ff[:, None] * fr, "e2m1")
    wbp = pack_weight(n((R, N)) * 1 / np.sqrt(R) / fr[:, None], "e2m1")
    return {
        "xt_words": xtp[0],
        "xt_scales": xtp[1],
        "xo_words": xop[0],
        "xo_scales": xop[1],
        "w_words": wp[0],
        "w_scales": wp[1],
        "w2_words": w2p[0],
        "w2_scales": w2p[1],
        "ca": e4m3fn_bytes(8.0 * n((R, V))),
        "cb": e4m3fn_bytes(8.0 * n((R, D))),
        "st": (np.random.uniform(0.01, 0.03, (R, 1)) * fr[:, None]).astype(np.float32),
        "wb_words": wbp[0],
        "wb_scales": wbp[1],
        "offs": striped(idx),
        "offs2": striped(idx2),
        "offs3": striped(idx3),
        "offs4": striped(idx4),
    }


def reference(xt_words, xt_scales, xo_words, xo_scales, w_words, w_scales, w2_words, w2_scales, ca, cb, st, wb_words, wb_scales, offs, offs2, offs3, offs4):
    idx = unstriped(offs)
    idx2 = unstriped(offs2)
    idx3 = unstriped(offs3)
    idx4 = unstriped(offs4)
    xtu = unpack_weight(xt_words, xt_scales, "e5m2")
    xou = unpack_weight(xo_words, xo_scales, "e4m3")
    wu = unpack_weight(w_words, w_scales, "e2m1")
    w2u = unpack_weight(w2_words, w2_scales, "e2m1")
    wbu = unpack_weight(wb_words, wb_scales, "e2m1")
    xtidxg = xtu[:, idx]
    a = wu.T @ xtidxg
    xoidx2g = xou[:, idx2]
    b = w2u.T @ xoidx2g
    g1 = e4m3fn_values(ca)[:, idx3] * e4m3fn_values(cb)[:, idx4] * f64(st)
    hid = np.maximum(a * g1, b)
    hidq = mxq(hid, 0, "e4m3")
    p = wbu.T @ hidq
    return p

@@ -1,0 +1,180 @@
+from contextlib import ExitStack
+
+import concourse.mybir as mybir
+
+K, T, J, R, F, Z, V, D, N = 512, 1024, 256, 512, 512, 1024, 1024, 512, 256
+FLOPS = 2 * J * (K * R + F * R + R * N)
+
+F32 = mybir.dt.float32
+BF16 = mybir.dt.bfloat16
+I32 = mybir.dt.int32
+U32 = mybir.dt.uint32
+U16 = mybir.dt.uint16
+U8 = mybir.dt.uint8
+E4M3 = mybir.dt.float8_e4m3fn
+E4M3X4 = mybir.dt.float8_e4m3fn_x4
+E5M2X4 = mybir.dt.float8_e5m2_x4
+E2M1X4 = mybir.dt.float4_e2m1fn_x4
+MULT = mybir.AluOpType.mult
+MAX = mybir.AluOpType.max
+COPY = mybir.ActivationFunctionType.Copy
+
+P = 128
+PACK = 4
+HALF = J // 2
+
+
+def tile_list_productentries_kernel(tc, xt_words, xt_scales, xo_words, xo_scales, w_words, w_scales, w2_words, w2_scales, ca, cb, st, wb_words, wb_scales, offs, offs2, offs3, offs4, out):
+    nc = tc.nc
+    with ExitStack() as ctx:
+        keep = ctx.enter_context(tc.tile_pool(name="keep", bufs=1))
+        psum = ctx.enter_context(tc.psum_pool(name="psum", bufs=1))
+
+        def sbuf(name, shape, dtype):
+            return keep.tile(shape, dtype, name=name, align_bytes=64)
+
+        def load_list(name, src):
+            tile = sbuf(name, [P, J // 16], U16)
+            nc.sync.dma_start(tile[:], src)
+            return tile
+
+        def zeroed_plane(name, width):
+            tile = sbuf(name, [P, width], U8)
+            nc.vector.memset(tile[:].bitcast(I32), 0)
+            return tile
+
+        def load_plane(queue, tile, src):
+            for q in range(4):
+                queue.dma_start(tile[32 * q : 32 * q + 4, :].bitcast(I32), src[0, 4 * q : 4 * q + 4, :].bitcast(I32))
+
+        def load_words(name, src, width, dtype):
+            tile = sbuf(name, [P, width], dtype)
+            nc.sync.dma_start(tile[:].bitcast(I32), src.bitcast(I32))
+            return tile
+
+        def load_rows(name, src, t):
+            tile = sbuf(name, [P, src.shape[1]], U8)
+            nc.sync.dma_start(tile[:], src.rearrange("(p t) c -> t p c", t=PACK)[t])
+            return tile
+
+        def gather(dst, window, offsets):
+            nc.vector.tensor_copy(dst, window[:].indirect(offsets[:]))
+
+        xt_plane = zeroed_plane("xt_plane", T)
+        w_plane = zeroed_plane("w_plane", R)
+        xo_plane = zeroed_plane("xo_plane", Z)
+        w2_plane = zeroed_plane("w2_plane", R)
+        wb_plane = zeroed_plane("wb_plane", N)
+
+        list4 = load_list("list4", offs4)
+        cb_rows = [load_rows("cb_rows%d" % t, cb, t) for t in range(PACK)]
+        list3 = load_list("list3", offs3)
+        ca_rows = [load_rows("ca_rows%d" % t, ca, t) for t in range(2)]
+        list1 = load_list("list1", offs)
+        xt_tab = load_words("xt_tab", xt_words[0].rearrange("p c r -> p (c r)"), T, U32)
+        load_plane(nc.sync, xt_plane, xt_scales)
+        step = sbuf("step", [P, PACK], F32)
+        nc.sync.dma_start(step[:], st.rearrange("(p t) o -> p (t o)", t=PACK))
+        w_tab = load_words("w_tab", w_words[0], 2 * R, U8)
+        load_plane(nc.sync, w_plane, w_scales)
+        list2 = load_list("list2", offs2)
+        xo_tab = load_words("xo_tab", xo_words[0].rearrange("p c r -> p (c r)"), Z, U32)
+        ca_rows = ca_rows + [load_rows("ca_rows%d" % t, ca, t) for t in range(2, PACK)]
+        load_plane(nc.sync, xo_plane, xo_scales)
+        w2_tab = load_words("w2_tab", w2_words[0], 2 * R, U8)
+        load_plane(nc.sync, w2_plane, w2_scales)
+        wb_tab = load_words("wb_tab", wb_words[0], 2 * N, U8)
+        load_plane(nc.sync, wb_plane, wb_scales)
+
+        def deal_words(name, tab):
+            tile = sbuf(name, [P, 2 * R], U8)
+            nc.scalar.copy(tile[:].bitcast(U16).rearrange("p (t m) -> p t m", t=PACK), tab[:].bitcast(U16).rearrange("p (m t) -> p t m", t=PACK))
+            return tile
+
+        def deal_plane(name, plane):
+            tile = sbuf(name, [P, R], U8)
+            nc.vector.tensor_copy(tile[:].rearrange("p (t m) -> p t m", t=PACK), plane[:].rearrange("p (m t) -> p t m", t=PACK))
+            return tile
+
+        ca_got = sbuf("ca_got", [P, PACK, J], U8)
+        cb_got = sbuf("cb_got", [P, PACK, J], U8)
+        ca_st = sbuf("ca_st", [P, PACK, J], F32)
+        xt_got = sbuf("xt_got", [P, J], U32)
+        xts_got = sbuf("xts_got", [P, J], U8)
+        xo_got = sbuf("xo_got", [P, J], U32)
+        xos_got = sbuf("xos_got", [P, J], U8)
+
+        def look_ca(t):
+            gather(ca_got[:, t, :], ca_rows[t], list3)
+            nc.scalar.activation(ca_st[:, t, :], ca_got[:, t, :].bitcast(E4M3), COPY, scale=step[:, t : t + 1])
+
+        def first_stage(name, words, plane, got, got_plane, fmt):
+            banks = []
+            for h in range(2):
+                bank = psum.tile([P, PACK, HALF], F32, name="%s%d" % (name, h))
+                cols = slice(h * HALF, (h + 1) * HALF)
+                for t in range(PACK):
+                    nc.tensor.matmul_mx(
+                        out=bank[:, t, :],
+                        lhsT=words[:, 2 * P * t : 2 * P * (t + 1)].bitcast(E2M1X4),
+                        lhsT_scale=plane[:, P * t : P * (t + 1)],
+                        rhs=got[:, cols].bitcast(fmt),
+                        rhs_scale=got_plane[:, cols],
+                        start=True,
+                        stop=True,
+                    )
+                banks.append(bank)
+            return banks
+
+        for t in range(PACK):
+            gather(cb_got[:, t, :], cb_rows[t], list4)
+        look_ca(0)
+        look_ca(1)
+        gather(xt_got[:], xt_tab, list1)
+        gather(xts_got[:], xt_plane, list1)
+        w_dealt = deal_words("w_dealt", w_tab)
+        ws_dealt = deal_plane("ws_dealt", w_plane)
+        a_banks = first_stage("a", w_dealt, ws_dealt, xt_got, xts_got, E5M2X4)
+        look_ca(2)
+        look_ca(3)
+        gather(xo_got[:], xo_tab, list2)
+        gather(xos_got[:], xo_plane, list2)
+        w2_dealt = deal_words("w2_dealt", w2_tab)
+        w2s_dealt = deal_plane("w2s_dealt", w2_plane)
+        b_banks = first_stage("b", w2_dealt, w2s_dealt, xo_got, xos_got, E4M3X4)
+
+        gain = sbuf("gain", [P, PACK, J], F32)
+        for u in range(2):
+            rows = slice(2 * u, 2 * u + 2)
+            nc.vector.tensor_tensor(gain[:, rows, :], cb_got[:, rows, :].bitcast(E4M3), ca_st[:, rows, :], MULT)
+
+        scaled = [sbuf("scaled%d" % h, [P, PACK, HALF], F32) for h in range(2)]
+        hid = [sbuf("hid%d" % h, [P, HALF, PACK], BF16) for h in range(2)]
+        codes = [sbuf("codes%d" % h, [P, HALF], U32) for h in range(2)]
+        hid_plane = [sbuf("hid_plane%d" % h, [P, HALF], U8) for h in range(2)]
+        for h in range(2):
+            nc.vector.tensor_tensor(scaled[h][:], a_banks[h][:], gain[:, :, h * HALF : (h + 1) * HALF], MULT)
+        for h in range(2):
+            nc.vector.tensor_tensor(hid[h][:], b_banks[h][:].rearrange("p t j -> p j t"), scaled[h][:].rearrange("p t j -> p j t"), MAX)
+        for h in range(2):
+            nc.vector.quantize_mx(out=codes[h][:].bitcast(E4M3X4), scales=hid_plane[h][:], in_=hid[h][:].rearrange("p j t -> p (j t)"))
+
+        out_view = out.rearrange("(g p) j -> p g j", p=P)
+        for h in range(2):
+            result = sbuf("result%d" % h, [P, 2, HALF], F32)
+            for g in range(2):
+                bank = psum.tile([P, HALF], F32, name="o%d%d" % (h, g))
+                nc.tensor.matmul_mx(
+                    out=bank[:],
+                    lhsT=wb_tab[:, 2 * P * g : 2 * P * (g + 1)].bitcast(E2M1X4),
+                    lhsT_scale=wb_plane[:, P * g : P * (g + 1)],
+                    rhs=codes[h][:].bitcast(E4M3X4),
+                    rhs_scale=hid_plane[h][:],
+                    start=True,
+                    stop=True,
+                )
+                if g == 0:
+                    nc.scalar.copy(result[:, g, :], bank[:])
+                else:
+                    nc.vector.tensor_copy(result[:, g, :], bank[:])
+            nc.sync.dma_start(out_view[:, :, h * HALF : (h + 1) * HALF], result[:])

@@ -38,14 +38,14 @@ def tile_list_productentries_kernel(tc, xt_words, xt_scales, xo_words, xo_scales
             nc.sync.dma_start(tile[:], src)
             return tile
 
-        def zeroed_plane(name, width):
+        def zeroed_plane(engine, name, width):
             tile = sbuf(name, [P, width], U8)
-            nc.vector.memset(tile[:].bitcast(I32), 0)
+            engine.memset(tile[:].bitcast(I32), 0)
             return tile
 
         def load_plane(queue, tile, src):
             for q in range(4):
-                queue.dma_start(tile[32 * q : 32 * q + 4, :].bitcast(I32), src[0, 4 * q : 4 * q + 4, :].bitcast(I32))
+                queue.dma_start(tile[q:P:32, :].bitcast(I32), src[0].rearrange("(g r) c -> r g c", r=4)[q].bitcast(I32))
 
         def load_words(name, src, width, dtype):
             tile = sbuf(name, [P, width], dtype)
@@ -60,29 +60,31 @@ def tile_list_productentries_kernel(tc, xt_words, xt_scales, xo_words, xo_scales
         def gather(dst, window, offsets):
             nc.vector.tensor_copy(dst, window[:].indirect(offsets[:]))
 
-        xt_plane = zeroed_plane("xt_plane", T)
-        w_plane = zeroed_plane("w_plane", R)
-        xo_plane = zeroed_plane("xo_plane", Z)
-        w2_plane = zeroed_plane("w2_plane", R)
-        wb_plane = zeroed_plane("wb_plane", N)
+        step = sbuf("step", [P, PACK], F32)
+        nc.gpsimd.dma_start(step[:], st.rearrange("(p t) o -> p (t o)", t=PACK))
+        w2_plane = zeroed_plane(nc.gpsimd, "w2_plane", R)
+        load_plane(nc.gpsimd, w2_plane, w2_scales)
+        xt_plane = zeroed_plane(nc.vector, "xt_plane", T)
+        w_plane = zeroed_plane(nc.vector, "w_plane", R)
+        xo_plane = zeroed_plane(nc.vector, "xo_plane", Z)
+        wb_plane = zeroed_plane(nc.vector, "wb_plane", N)
 
         list4 = load_list("list4", offs4)
-        cb_rows = [load_rows("cb_rows%d" % t, cb, t) for t in range(PACK)]
+        cb_rows = [load_rows("cb_rows0", cb, 0)]
         list3 = load_list("list3", offs3)
-        ca_rows = [load_rows("ca_rows%d" % t, ca, t) for t in range(2)]
+        ca_rows = [load_rows("ca_rows0", ca, 0)]
+        for t in range(1, PACK):
+            cb_rows.append(load_rows("cb_rows%d" % t, cb, t))
+            ca_rows.append(load_rows("ca_rows%d" % t, ca, t))
         list1 = load_list("list1", offs)
         xt_tab = load_words("xt_tab", xt_words[0].rearrange("p c r -> p (c r)"), T, U32)
         load_plane(nc.sync, xt_plane, xt_scales)
-        step = sbuf("step", [P, PACK], F32)
-        nc.sync.dma_start(step[:], st.rearrange("(p t) o -> p (t o)", t=PACK))
         w_tab = load_words("w_tab", w_words[0], 2 * R, U8)
         load_plane(nc.sync, w_plane, w_scales)
         list2 = load_list("list2", offs2)
         xo_tab = load_words("xo_tab", xo_words[0].rearrange("p c r -> p (c r)"), Z, U32)
-        ca_rows = ca_rows + [load_rows("ca_rows%d" % t, ca, t) for t in range(2, PACK)]
-        load_plane(nc.sync, xo_plane, xo_scales)
         w2_tab = load_words("w2_tab", w2_words[0], 2 * R, U8)
-        load_plane(nc.sync, w2_plane, w2_scales)
+        load_plane(nc.sync, xo_plane, xo_scales)
         wb_tab = load_words("wb_tab", wb_words[0], 2 * N, U8)
         load_plane(nc.sync, wb_plane, wb_scales)
 
@@ -104,9 +106,15 @@ def tile_list_productentries_kernel(tc, xt_words, xt_scales, xo_words, xo_scales
         xo_got = sbuf("xo_got", [P, J], U32)
         xos_got = sbuf("xos_got", [P, J], U8)
 
-        def look_ca(t):
+        cb_val = sbuf("cb_val", [P, PACK, J], F32)
+        gain = sbuf("gain", [P, PACK, J], F32)
+
+        def look_up(t):
+            gather(cb_got[:, t, :], cb_rows[t], list4)
+            nc.scalar.copy(cb_val[:, t, :], cb_got[:, t, :].bitcast(E4M3))
             gather(ca_got[:, t, :], ca_rows[t], list3)
             nc.scalar.activation(ca_st[:, t, :], ca_got[:, t, :].bitcast(E4M3), COPY, scale=step[:, t : t + 1])
+            nc.gpsimd.tensor_tensor(gain[:, t, :], cb_val[:, t, :], ca_st[:, t, :], MULT)
 
         def first_stage(name, words, plane, got, got_plane, fmt):
             banks = []
@@ -127,26 +135,17 @@ def tile_list_productentries_kernel(tc, xt_words, xt_scales, xo_words, xo_scales
             return banks
 
         for t in range(PACK):
-            gather(cb_got[:, t, :], cb_rows[t], list4)
-        look_ca(0)
-        look_ca(1)
+            look_up(t)
         gather(xt_got[:], xt_tab, list1)
         gather(xts_got[:], xt_plane, list1)
         w_dealt = deal_words("w_dealt", w_tab)
         ws_dealt = deal_plane("ws_dealt", w_plane)
         a_banks = first_stage("a", w_dealt, ws_dealt, xt_got, xts_got, E5M2X4)
-        look_ca(2)
-        look_ca(3)
         gather(xo_got[:], xo_tab, list2)
         gather(xos_got[:], xo_plane, list2)
         w2_dealt = deal_words("w2_dealt", w2_tab)
         w2s_dealt = deal_plane("w2s_dealt", w2_plane)
         b_banks = first_stage("b", w2_dealt, w2s_dealt, xo_got, xos_got, E4M3X4)
-
-        gain = sbuf("gain", [P, PACK, J], F32)
-        for u in range(2):
-            rows = slice(2 * u, 2 * u + 2)
-            nc.vector.tensor_tensor(gain[:, rows, :], cb_got[:, rows, :].bitcast(E4M3), ca_st[:, rows, :], MULT)
 
         scaled = [sbuf("scaled%d" % h, [P, PACK, HALF], F32) for h in range(2)]
         hid = [sbuf("hid%d" % h, [P, HALF, PACK], BF16) for h in range(2)]

@@ -30,8 +30,8 @@ def tile_list_productentries_kernel(tc, xt_words, xt_scales, xo_words, xo_scales
         keep = ctx.enter_context(tc.tile_pool(name="keep", bufs=1))
         psum = ctx.enter_context(tc.psum_pool(name="psum", bufs=1))
 
-        def sbuf(name, shape, dtype):
-            return keep.tile(shape, dtype, name=name, align_bytes=64)
+        def sbuf(name, shape, dtype, tag=None):
+            return keep.tile(shape, dtype, name=name, tag=tag or name, align_bytes=64)
 
         def load_list(name, src):
             tile = sbuf(name, [P, J // 16], U16)
@@ -45,7 +45,7 @@ def tile_list_productentries_kernel(tc, xt_words, xt_scales, xo_words, xo_scales
 
         def load_plane(queue, tile, src):
             for q in range(4):
-                queue.dma_start(tile[q:P:32, :].bitcast(I32), src[0].rearrange("(g r) c -> r g c", r=4)[q].bitcast(I32))
+                queue.dma_start(tile[32 * q : 32 * q + 4, :].bitcast(I32), src[0, 4 * q : 4 * q + 4, :].bitcast(I32))
 
         def load_words(name, src, width, dtype):
             tile = sbuf(name, [P, width], dtype)
@@ -62,11 +62,11 @@ def tile_list_productentries_kernel(tc, xt_words, xt_scales, xo_words, xo_scales
 
         step = sbuf("step", [P, PACK], F32)
         nc.gpsimd.dma_start(step[:], st.rearrange("(p t) o -> p (t o)", t=PACK))
-        w2_plane = zeroed_plane(nc.gpsimd, "w2_plane", R)
-        load_plane(nc.gpsimd, w2_plane, w2_scales)
+        xo_plane = zeroed_plane(nc.vector, "xo_plane", Z)
+        load_plane(nc.gpsimd, xo_plane, xo_scales)
         xt_plane = zeroed_plane(nc.vector, "xt_plane", T)
         w_plane = zeroed_plane(nc.vector, "w_plane", R)
-        xo_plane = zeroed_plane(nc.vector, "xo_plane", Z)
+        w2_plane = zeroed_plane(nc.vector, "w2_plane", R)
         wb_plane = zeroed_plane(nc.vector, "wb_plane", N)
 
         list4 = load_list("list4", offs4)
@@ -81,10 +81,10 @@ def tile_list_productentries_kernel(tc, xt_words, xt_scales, xo_words, xo_scales
         load_plane(nc.sync, xt_plane, xt_scales)
         w_tab = load_words("w_tab", w_words[0], 2 * R, U8)
         load_plane(nc.sync, w_plane, w_scales)
-        list2 = load_list("list2", offs2)
         xo_tab = load_words("xo_tab", xo_words[0].rearrange("p c r -> p (c r)"), Z, U32)
+        list2 = load_list("list2", offs2)
         w2_tab = load_words("w2_tab", w2_words[0], 2 * R, U8)
-        load_plane(nc.sync, xo_plane, xo_scales)
+        load_plane(nc.sync, w2_plane, w2_scales)
         wb_tab = load_words("wb_tab", wb_words[0], 2 * N, U8)
         load_plane(nc.sync, wb_plane, wb_scales)
 
@@ -147,21 +147,26 @@ def tile_list_productentries_kernel(tc, xt_words, xt_scales, xo_words, xo_scales
         w2s_dealt = deal_plane("w2s_dealt", w2_plane)
         b_banks = first_stage("b", w2_dealt, w2s_dealt, xo_got, xos_got, E4M3X4)
 
-        scaled = [sbuf("scaled%d" % h, [P, PACK, HALF], F32) for h in range(2)]
+        scaled = [sbuf("scaled%d" % h, [P, PACK, HALF], F32, tag=("xo_plane", "w2_plane")[h]) for h in range(2)]
         hid = [sbuf("hid%d" % h, [P, HALF, PACK], BF16) for h in range(2)]
         codes = [sbuf("codes%d" % h, [P, HALF], U32) for h in range(2)]
         hid_plane = [sbuf("hid_plane%d" % h, [P, HALF], U8) for h in range(2)]
         for h in range(2):
             nc.vector.tensor_tensor(scaled[h][:], a_banks[h][:], gain[:, :, h * HALF : (h + 1) * HALF], MULT)
         for h in range(2):
-            nc.vector.tensor_tensor(hid[h][:], b_banks[h][:].rearrange("p t j -> p j t"), scaled[h][:].rearrange("p t j -> p j t"), MAX)
+            nc.vector.tensor_tensor(
+                hid[h][:].rearrange("p (c i) t -> p c t i", i=4),
+                b_banks[h][:].rearrange("p t (c i) -> p c t i", i=4),
+                scaled[h][:].rearrange("p t (c i) -> p c t i", i=4),
+                MAX,
+            )
         for h in range(2):
             nc.vector.quantize_mx(out=codes[h][:].bitcast(E4M3X4), scales=hid_plane[h][:], in_=hid[h][:].rearrange("p j t -> p (j t)"))
 
         out_view = out.rearrange("(g p) j -> p g j", p=P)
         for h in range(2):
-            result = sbuf("result%d" % h, [P, 2, HALF], F32)
             for g in range(2):
+                result = sbuf("result%d%d" % (h, g), [P, HALF], F32)
                 bank = psum.tile([P, HALF], F32, name="o%d%d" % (h, g))
                 nc.tensor.matmul_mx(
                     out=bank[:],
@@ -173,7 +178,8 @@ def tile_list_productentries_kernel(tc, xt_words, xt_scales, xo_words, xo_scales
                     stop=True,
                 )
                 if g == 0:
-                    nc.scalar.copy(result[:, g, :], bank[:])
+                    nc.scalar.copy(result[:], bank[:])
+                    nc.scalar.dma_start(out_view[:, g, h * HALF : (h + 1) * HALF], result[:])
                 else:
-                    nc.vector.tensor_copy(result[:, g, :], bank[:])
-            nc.sync.dma_start(out_view[:, :, h * HALF : (h + 1) * HALF], result[:])
+                    nc.vector.tensor_copy(result[:], bank[:])
+                    nc.sync.dma_start(out_view[:, g, h * HALF : (h + 1) * HALF], result[:])

@@ -93,8 +93,8 @@ def tile_list_productentries_kernel(tc, xt_words, xt_scales, xo_words, xo_scales
             nc.scalar.copy(tile[:].bitcast(U16).rearrange("p (t m) -> p t m", t=PACK), tab[:].bitcast(U16).rearrange("p (m t) -> p t m", t=PACK))
             return tile
 
-        def deal_plane(name, plane):
-            tile = sbuf(name, [P, R], U8)
+        def deal_plane(name, plane, tag=None):
+            tile = sbuf(name, [P, R], U8, tag=tag)
             nc.vector.tensor_copy(tile[:].rearrange("p (t m) -> p t m", t=PACK), plane[:].rearrange("p (m t) -> p t m", t=PACK))
             return tile
 
@@ -144,20 +144,20 @@ def tile_list_productentries_kernel(tc, xt_words, xt_scales, xo_words, xo_scales
         gather(xo_got[:], xo_tab, list2)
         gather(xos_got[:], xo_plane, list2)
         w2_dealt = deal_words("w2_dealt", w2_tab)
-        w2s_dealt = deal_plane("w2s_dealt", w2_plane)
+        w2s_dealt = deal_plane("w2s_dealt", w2_plane, tag="xo_plane")
         b_banks = first_stage("b", w2_dealt, w2s_dealt, xo_got, xos_got, E4M3X4)
 
-        scaled = [sbuf("scaled%d" % h, [P, PACK, HALF], F32, tag=("xo_plane", "w2_plane")[h]) for h in range(2)]
+        scaled = sbuf("scaled", [P, 2, PACK, HALF], F32, tag="w2_plane")
         hid = [sbuf("hid%d" % h, [P, HALF, PACK], BF16) for h in range(2)]
         codes = [sbuf("codes%d" % h, [P, HALF], U32) for h in range(2)]
         hid_plane = [sbuf("hid_plane%d" % h, [P, HALF], U8) for h in range(2)]
         for h in range(2):
-            nc.vector.tensor_tensor(scaled[h][:], a_banks[h][:], gain[:, :, h * HALF : (h + 1) * HALF], MULT)
+            nc.vector.tensor_tensor(scaled[:, h], a_banks[h][:], gain[:, :, h * HALF : (h + 1) * HALF], MULT)
         for h in range(2):
             nc.vector.tensor_tensor(
                 hid[h][:].rearrange("p (c i) t -> p c t i", i=4),
                 b_banks[h][:].rearrange("p t (c i) -> p c t i", i=4),
-                scaled[h][:].rearrange("p t (c i) -> p c t i", i=4),
+                scaled[:, h].rearrange("p t (c i) -> p c t i", i=4),
                 MAX,
             )
         for h in range(2):

@@ -60,8 +60,6 @@ def tile_list_productentries_kernel(tc, xt_words, xt_scales, xo_words, xo_scales
         def gather(dst, window, offsets):
             nc.vector.tensor_copy(dst, window[:].indirect(offsets[:]))
 
-        step = sbuf("step", [P, PACK], F32)
-        nc.gpsimd.dma_start(step[:], st.rearrange("(p t) o -> p (t o)", t=PACK))
         xo_plane = zeroed_plane(nc.vector, "xo_plane", Z)
         load_plane(nc.gpsimd, xo_plane, xo_scales)
         xt_plane = zeroed_plane(nc.vector, "xt_plane", T)
@@ -73,16 +71,18 @@ def tile_list_productentries_kernel(tc, xt_words, xt_scales, xo_words, xo_scales
         cb_rows = [load_rows("cb_rows0", cb, 0)]
         list3 = load_list("list3", offs3)
         ca_rows = [load_rows("ca_rows0", ca, 0)]
+        step = sbuf("step", [P, PACK], F32)
+        nc.sync.dma_start(step[:], st.rearrange("(p t) o -> p (t o)", t=PACK))
         for t in range(1, PACK):
             cb_rows.append(load_rows("cb_rows%d" % t, cb, t))
             ca_rows.append(load_rows("ca_rows%d" % t, ca, t))
         list1 = load_list("list1", offs)
-        xt_tab = load_words("xt_tab", xt_words[0].rearrange("p c r -> p (c r)"), T, U32)
         load_plane(nc.sync, xt_plane, xt_scales)
+        xt_tab = load_words("xt_tab", xt_words[0].rearrange("p c r -> p (c r)"), T, U32)
         w_tab = load_words("w_tab", w_words[0], 2 * R, U8)
         load_plane(nc.sync, w_plane, w_scales)
-        xo_tab = load_words("xo_tab", xo_words[0].rearrange("p c r -> p (c r)"), Z, U32)
         list2 = load_list("list2", offs2)
+        xo_tab = load_words("xo_tab", xo_words[0].rearrange("p c r -> p (c r)"), Z, U32)
         w2_tab = load_words("w2_tab", w2_words[0], 2 * R, U8)
         load_plane(nc.sync, w2_plane, w2_scales)
         wb_tab = load_words("wb_tab", wb_words[0], 2 * N, U8)
@@ -93,14 +93,13 @@ def tile_list_productentries_kernel(tc, xt_words, xt_scales, xo_words, xo_scales
             nc.scalar.copy(tile[:].bitcast(U16).rearrange("p (t m) -> p t m", t=PACK), tab[:].bitcast(U16).rearrange("p (m t) -> p t m", t=PACK))
             return tile
 
-        def deal_plane(name, plane, tag=None):
+        def deal_plane(engine, name, plane, tag=None):
             tile = sbuf(name, [P, R], U8, tag=tag)
-            nc.vector.tensor_copy(tile[:].rearrange("p (t m) -> p t m", t=PACK), plane[:].rearrange("p (m t) -> p t m", t=PACK))
+            engine.tensor_copy(tile[:].rearrange("p (t m) -> p t m", t=PACK), plane[:].rearrange("p (m t) -> p t m", t=PACK))
             return tile
 
         ca_got = sbuf("ca_got", [P, PACK, J], U8)
         cb_got = sbuf("cb_got", [P, PACK, J], U8)
-        ca_st = sbuf("ca_st", [P, PACK, J], F32)
         xt_got = sbuf("xt_got", [P, J], U32)
         xts_got = sbuf("xts_got", [P, J], U8)
         xo_got = sbuf("xo_got", [P, J], U32)
@@ -113,8 +112,9 @@ def tile_list_productentries_kernel(tc, xt_words, xt_scales, xo_words, xo_scales
             gather(cb_got[:, t, :], cb_rows[t], list4)
             nc.scalar.copy(cb_val[:, t, :], cb_got[:, t, :].bitcast(E4M3))
             gather(ca_got[:, t, :], ca_rows[t], list3)
-            nc.scalar.activation(ca_st[:, t, :], ca_got[:, t, :].bitcast(E4M3), COPY, scale=step[:, t : t + 1])
-            nc.gpsimd.tensor_tensor(gain[:, t, :], cb_val[:, t, :], ca_st[:, t, :], MULT)
+            ca_st = sbuf("ca_st%d" % t, [P, J], F32, tag="w_plane" if t == PACK - 1 else None)
+            nc.scalar.activation(ca_st[:], ca_got[:, t, :].bitcast(E4M3), COPY, scale=step[:, t : t + 1])
+            nc.gpsimd.tensor_tensor(gain[:, t, :], cb_val[:, t, :], ca_st[:], MULT)
 
         def first_stage(name, words, plane, got, got_plane, fmt):
             banks = []
@@ -134,17 +134,17 @@ def tile_list_productentries_kernel(tc, xt_words, xt_scales, xo_words, xo_scales
                 banks.append(bank)
             return banks
 
+        ws_dealt = deal_plane(nc.gpsimd, "ws_dealt", w_plane)
         for t in range(PACK):
             look_up(t)
         gather(xt_got[:], xt_tab, list1)
         gather(xts_got[:], xt_plane, list1)
         w_dealt = deal_words("w_dealt", w_tab)
-        ws_dealt = deal_plane("ws_dealt", w_plane)
         a_banks = first_stage("a", w_dealt, ws_dealt, xt_got, xts_got, E5M2X4)
         gather(xo_got[:], xo_tab, list2)
         gather(xos_got[:], xo_plane, list2)
         w2_dealt = deal_words("w2_dealt", w2_tab)
-        w2s_dealt = deal_plane("w2s_dealt", w2_plane, tag="xo_plane")
+        w2s_dealt = deal_plane(nc.vector, "w2s_dealt", w2_plane, tag="xo_plane")
         b_banks = first_stage("b", w2_dealt, w2s_dealt, xo_got, xos_got, E4M3X4)
 
         scaled = sbuf("scaled", [P, 2, PACK, HALF], F32, tag="w2_plane")

from contextlib import ExitStack

import concourse.mybir as mybir

K, T, J, R, F, Z, V, D, N = 512, 1024, 256, 512, 512, 1024, 1024, 512, 256
FLOPS = 2 * J * (K * R + F * R + R * N)

F32 = mybir.dt.float32
BF16 = mybir.dt.bfloat16
I32 = mybir.dt.int32
U32 = mybir.dt.uint32
U16 = mybir.dt.uint16
U8 = mybir.dt.uint8
E4M3 = mybir.dt.float8_e4m3fn
E4M3X4 = mybir.dt.float8_e4m3fn_x4
E5M2X4 = mybir.dt.float8_e5m2_x4
E2M1X4 = mybir.dt.float4_e2m1fn_x4
MULT = mybir.AluOpType.mult
MAX = mybir.AluOpType.max
COPY = mybir.ActivationFunctionType.Copy

P = 128
PACK = 4
HALF = J // 2


def tile_list_productentries_kernel(tc, xt_words, xt_scales, xo_words, xo_scales, w_words, w_scales, w2_words, w2_scales, ca, cb, st, wb_words, wb_scales, offs, offs2, offs3, offs4, out):
    nc = tc.nc
    with ExitStack() as ctx:
        keep = ctx.enter_context(tc.tile_pool(name="keep", bufs=1))
        psum = ctx.enter_context(tc.psum_pool(name="psum", bufs=1))

        def sbuf(name, shape, dtype, tag=None):
            return keep.tile(shape, dtype, name=name, tag=tag or name, align_bytes=64)

        def load_list(name, src):
            tile = sbuf(name, [P, J // 16], U16)
            nc.sync.dma_start(tile[:], src)
            return tile

        def zeroed_plane(engine, name, width):
            tile = sbuf(name, [P, width], U8)
            engine.memset(tile[:].bitcast(I32), 0)
            return tile

        def load_plane(queue, tile, src):
            for q in range(4):
                queue.dma_start(tile[32 * q : 32 * q + 4, :].bitcast(I32), src[0, 4 * q : 4 * q + 4, :].bitcast(I32))

        def load_words(name, src, width, dtype):
            tile = sbuf(name, [P, width], dtype)
            nc.sync.dma_start(tile[:].bitcast(I32), src.bitcast(I32))
            return tile

        def load_rows(name, src, t):
            tile = sbuf(name, [P, src.shape[1]], U8)
            nc.sync.dma_start(tile[:], src.rearrange("(p t) c -> t p c", t=PACK)[t])
            return tile

        def gather(dst, window, offsets):
            nc.vector.tensor_copy(dst, window[:].indirect(offsets[:]))

        xo_plane = zeroed_plane(nc.vector, "xo_plane", Z)
        load_plane(nc.gpsimd, xo_plane, xo_scales)
        xt_plane = zeroed_plane(nc.vector, "xt_plane", T)
        w_plane = zeroed_plane(nc.vector, "w_plane", R)
        w2_plane = zeroed_plane(nc.vector, "w2_plane", R)
        wb_plane = zeroed_plane(nc.vector, "wb_plane", N)

        list4 = load_list("list4", offs4)
        cb_rows = [load_rows("cb_rows0", cb, 0)]
        list3 = load_list("list3", offs3)
        ca_rows = [load_rows("ca_rows0", ca, 0)]
        step = sbuf("step", [P, PACK], F32)
        nc.sync.dma_start(step[:], st.rearrange("(p t) o -> p (t o)", t=PACK))
        for t in range(1, PACK):
            cb_rows.append(load_rows("cb_rows%d" % t, cb, t))
            ca_rows.append(load_rows("ca_rows%d" % t, ca, t))
        list1 = load_list("list1", offs)
        load_plane(nc.sync, xt_plane, xt_scales)
        xt_tab = load_words("xt_tab", xt_words[0].rearrange("p c r -> p (c r)"), T, U32)
        w_tab = load_words("w_tab", w_words[0], 2 * R, U8)
        load_plane(nc.sync, w_plane, w_scales)
        list2 = load_list("list2", offs2)
        xo_tab = load_words("xo_tab", xo_words[0].rearrange("p c r -> p (c r)"), Z, U32)
        w2_tab = load_words("w2_tab", w2_words[0], 2 * R, U8)
        load_plane(nc.sync, w2_plane, w2_scales)
        wb_tab = load_words("wb_tab", wb_words[0], 2 * N, U8)
        load_plane(nc.sync, wb_plane, wb_scales)

        def deal_words(name, tab):
            tile = sbuf(name, [P, 2 * R], U8)
            nc.scalar.copy(tile[:].bitcast(U16).rearrange("p (t m) -> p t m", t=PACK), tab[:].bitcast(U16).rearrange("p (m t) -> p t m", t=PACK))
            return tile

        def deal_plane(engine, name, plane, tag=None):
            tile = sbuf(name, [P, R], U8, tag=tag)
            engine.tensor_copy(tile[:].rearrange("p (t m) -> p t m", t=PACK), plane[:].rearrange("p (m t) -> p t m", t=PACK))
            return tile

        ca_got = sbuf("ca_got", [P, PACK, J], U8)
        cb_got = sbuf("cb_got", [P, PACK, J], U8)
        xt_got = sbuf("xt_got", [P, J], U32)
        xts_got = sbuf("xts_got", [P, J], U8)
        xo_got = sbuf("xo_got", [P, J], U32)
        xos_got = sbuf("xos_got", [P, J], U8)

        cb_val = sbuf("cb_val", [P, PACK, J], F32)
        gain = sbuf("gain", [P, PACK, J], F32)

        def look_up(t):
            gather(cb_got[:, t, :], cb_rows[t], list4)
            nc.scalar.copy(cb_val[:, t, :], cb_got[:, t, :].bitcast(E4M3))
            gather(ca_got[:, t, :], ca_rows[t], list3)
            ca_st = sbuf("ca_st%d" % t, [P, J], F32, tag="w_plane" if t == PACK - 1 else None)
            nc.scalar.activation(ca_st[:], ca_got[:, t, :].bitcast(E4M3), COPY, scale=step[:, t : t + 1])
            nc.gpsimd.tensor_tensor(gain[:, t, :], cb_val[:, t, :], ca_st[:], MULT)

        def first_stage(name, words, plane, got, got_plane, fmt):
            banks = []
            for h in range(2):
                bank = psum.tile([P, PACK, HALF], F32, name="%s%d" % (name, h))
                cols = slice(h * HALF, (h + 1) * HALF)
                for t in range(PACK):
                    nc.tensor.matmul_mx(
                        out=bank[:, t, :],
                        lhsT=words[:, 2 * P * t : 2 * P * (t + 1)].bitcast(E2M1X4),
                        lhsT_scale=plane[:, P * t : P * (t + 1)],
                        rhs=got[:, cols].bitcast(fmt),
                        rhs_scale=got_plane[:, cols],
                        start=True,
                        stop=True,
                    )
                banks.append(bank)
            return banks

        ws_dealt = deal_plane(nc.gpsimd, "ws_dealt", w_plane)
        for t in range(PACK):
            look_up(t)
        gather(xt_got[:], xt_tab, list1)
        gather(xts_got[:], xt_plane, list1)
        w_dealt = deal_words("w_dealt", w_tab)
        a_banks = first_stage("a", w_dealt, ws_dealt, xt_got, xts_got, E5M2X4)
        gather(xo_got[:], xo_tab, list2)
        gather(xos_got[:], xo_plane, list2)
        w2_dealt = deal_words("w2_dealt", w2_tab)
        w2s_dealt = deal_plane(nc.vector, "w2s_dealt", w2_plane, tag="xo_plane")
        b_banks = first_stage("b", w2_dealt, w2s_dealt, xo_got, xos_got, E4M3X4)

        scaled = sbuf("scaled", [P, 2, PACK, HALF], F32, tag="w2_plane")
        hid = [sbuf("hid%d" % h, [P, HALF, PACK], BF16) for h in range(2)]
        codes = [sbuf("codes%d" % h, [P, HALF], U32) for h in range(2)]
        hid_plane = [sbuf("hid_plane%d" % h, [P, HALF], U8) for h in range(2)]
        for h in range(2):
            nc.vector.tensor_tensor(scaled[:, h], a_banks[h][:], gain[:, :, h * HALF : (h + 1) * HALF], MULT)
        for h in range(2):
            nc.vector.tensor_tensor(
                hid[h][:].rearrange("p (c i) t -> p c t i", i=4),
                b_banks[h][:].rearrange("p t (c i) -> p c t i", i=4),
                scaled[:, h].rearrange("p t (c i) -> p c t i", i=4),
                MAX,
            )
        for h in range(2):
            nc.vector.quantize_mx(out=codes[h][:].bitcast(E4M3X4), scales=hid_plane[h][:], in_=hid[h][:].rearrange("p j t -> p (j t)"))

        out_view = out.rearrange("(g p) j -> p g j", p=P)
        for h in range(2):
            for g in range(2):
                result = sbuf("result%d%d" % (h, g), [P, HALF], F32)
                bank = psum.tile([P, HALF], F32, name="o%d%d" % (h, g))
                nc.tensor.matmul_mx(
                    out=bank[:],
                    lhsT=wb_tab[:, 2 * P * g : 2 * P * (g + 1)].bitcast(E2M1X4),
                    lhsT_scale=wb_plane[:, P * g : P * (g + 1)],
                    rhs=codes[h][:].bitcast(E4M3X4),
                    rhs_scale=hid_plane[h][:],
                    start=True,
                    stop=True,
                )
                if g == 0:
                    nc.scalar.copy(result[:], bank[:])
                    nc.scalar.dma_start(out_view[:, g, h * HALF : (h + 1) * HALF], result[:])
                else:
                    nc.vector.tensor_copy(result[:], bank[:])
                    nc.sync.dma_start(out_view[:, g, h * HALF : (h + 1) * HALF], result[:])
